import numpy as np
import ml_dtypes


def mxq(x, axis, fmt="e4m3"):
    dtype, down = {"e4m3": (ml_dtypes.float8_e4m3fn, 7), "e5m2": (ml_dtypes.float8_e5m2, 14)}[fmt]
    v = np.moveaxis(np.asarray(x, np.float32).astype(ml_dtypes.bfloat16).astype(np.float64), axis, -1)
    blocks = v.reshape(v.shape[:-1] + (-1, 32))
    amax = np.abs(blocks).max(-1, keepdims=True)
    byte = np.maximum(np.where(amax > 0, np.frexp(amax)[1] - 1 + 127, 0) - down, 1)
    scale = np.exp2(byte - 127.0)
    codes = (blocks / scale).astype(np.float32).astype(dtype).astype(np.float64)
    return np.moveaxis((codes * scale).reshape(v.shape), -1, axis)


WIDE = False


def mx_kscale(k):
    if not WIDE:
        return np.ones(k)
    levels = np.array([30, -30])
    if k % 512:
        return np.exp2(np.random.permutation(np.resize(levels, k // 32))).repeat(32)
    a = np.empty((k // 512, 16))
    for p in range(k // 512):
        a[p, :8] = np.random.permutation(np.resize(levels, 8))
        for g in range(8):
            far = levels[np.abs(levels - a[p, g]) >= 10]
            a[p, g + 8] = far[np.random.randint(len(far))]
    return np.exp2(a.ravel()).repeat(32)


def f64(x):
    return np.asarray(x).astype(np.float64)


def striped(idx):
    return np.tile(np.asarray(idx).reshape(-1, 16).T, (8, 1)).astype(np.uint16)


def unstriped(offs):
    return offs[:16].T.reshape(-1).astype(np.int64)


E2M1 = np.array([0.0, 0.5, 1.0, 1.5, 2.0, 3.0, 4.0, 6.0, -0.0, -0.5, -1.0, -1.5, -2.0, -3.0, -4.0, -6.0])


def pack_weight(w, fmt):
    k, n = w.shape
    w = f64(np.asarray(w, np.float32).astype(ml_dtypes.bfloat16)).reshape(k // 32, 32, n)
    amax = np.abs(w).max(1)
    if fmt in ("e4m3", "e5m2"):
        byte = np.frexp(amax)[1] - 1 + 127 - (7 if fmt == "e4m3" else 14)
    else:
        mant, ex = np.frexp(amax / 6.0)
        byte = np.where(mant > 0.5, ex, ex - 1) + 127
    byte = np.clip(np.where(amax > 0, byte, 1), 1, 254)
    scaled = (w * np.exp2(127.0 - byte)[:, None, :]).reshape(k, n).astype(np.float32)
    by_word = np.ascontiguousarray(scaled.reshape(k // 512, 128, 4, n).transpose(0, 1, 3, 2))
    if fmt in ("e4m3", "e5m2"):
        words = by_word.astype(ml_dtypes.float8_e4m3fn if fmt == "e4m3" else ml_dtypes.float8_e5m2).view(np.uint8)
    else:
        c = by_word.astype(ml_dtypes.float4_e2m1fn).view(np.uint8) & 0xF
        words = (c[..., 0::2] | (c[..., 1::2] << 4)).reshape(k // 512, 128, 2 * n)
    return np.ascontiguousarray(words), np.ascontiguousarray(byte.astype(np.uint8).reshape(k // 512, 16, n))


def unpack_weight(words, scales, fmt):
    g, _, n = scales.shape
    words = np.ascontiguousarray(words).reshape(g, 128, n, -1)
    if fmt in ("e4m3", "e5m2"):
        vals = words.view(ml_dtypes.float8_e4m3fn if fmt == "e4m3" else ml_dtypes.float8_e5m2).astype(np.float64)
    else:
        nib = np.empty((g, 128, n, 4), np.uint8)
        nib[..., 0::2] = words & 0xF
        nib[..., 1::2] = words >> 4
        vals = E2M1[nib]
    vals = vals * np.repeat(np.exp2(scales.astype(np.float64) - 127.0), 8, axis=1)[..., None]
    return vals.transpose(0, 1, 3, 2).reshape(g * 512, n)


def sigmoid(v):
    return 1.0 / (1.0 + np.exp(-v))


K, T, J, R, O, N, E = 512, 1024, 256, 512, 128, 256, 1024


def setup_inputs():
    n = np.random.standard_normal
    idx = np.random.permutation(T)[:J]
    idx2 = np.random.permutation(J)[:O]
    idx3 = np.random.permutation(J)[:O]
    idx4 = np.random.permutation(E)[:O]
    fk = mx_kscale(K)
    fr = mx_kscale(R)
    xtp = pack_weight(n((K, T)) / fk[:, None], "e4m3")
    wp = pack_weight(n((K, R)) * 1 / np.sqrt(K) * fk[:, None], "e2m1")
    w2p = pack_weight(n((K, R)) * 1 / np.sqrt(K) * fk[:, None] * fr, "e5m2")
    wbp = pack_weight(n((R, N)) * 1 / np.sqrt(R) / fr[:, None], "e5m2")
    return {
        "xt_words": xtp[0],
        "xt_scales": xtp[1],
        "w_words": wp[0],
        "w_scales": wp[1],
        "w2_words": w2p[0],
        "w2_scales": w2p[1],
        "sg": (np.random.uniform(0.6, 1.6, (R, 1))).astype(np.float32),
        "bg": (np.random.uniform(-1.0, 1.0, (R, 1))).astype(np.float32),
        "wb_words": wbp[0],
        "wb_scales": wbp[1],
        "offs": striped(idx),
        "offs2": striped(idx2),
        "offs3": striped(idx3),
        "offs4": striped(idx4),
    }


def reference(xt_words, xt_scales, w_words, w_scales, w2_words, w2_scales, sg, bg, wb_words, wb_scales, offs, offs2, offs3, offs4):
    idx = unstriped(offs)
    idx2 = unstriped(offs2)
    idx3 = unstriped(offs3)
    idx4 = unstriped(offs4)
    xtu = unpack_weight(xt_words, xt_scales, "e4m3")
    wu = unpack_weight(w_words, w_scales, "e2m1")
    w2u = unpack_weight(w2_words, w2_scales, "e5m2")
    wbu = unpack_weight(wb_words, wb_scales, "e5m2")
    xtidxg = xtu[:, idx]
    a = wu.T @ xtidxg
    b = w2u.T @ xtidxg
    hid = b[:, idx3] * sigmoid(a[:, idx2] * f64(sg) + f64(bg))
    hidq = mxq(hid, 0, "e4m3")
    p = wbu.T @ hidq
    y = np.zeros((N, E))
    y[:, idx4] = p
    return y

@@ -1,0 +1,175 @@
+from contextlib import ExitStack
+
+import concourse.mybir as mybir
+
+K, T, J, R, O, N, E = 512, 1024, 256, 512, 128, 256, 1024
+FLOPS = 2 * K * R * J * 2 + 2 * R * N * O
+
+F32 = mybir.dt.float32
+BF16 = mybir.dt.bfloat16
+I32 = mybir.dt.int32
+U32 = mybir.dt.uint32
+U16 = mybir.dt.uint16
+U8 = mybir.dt.uint8
+E4M3 = mybir.dt.float8_e4m3fn_x4
+E5M2 = mybir.dt.float8_e5m2_x4
+E2M1 = mybir.dt.float4_e2m1fn_x4
+ACT = mybir.ActivationFunctionType
+MULT = mybir.AluOpType.mult
+P = 128
+PACK = 4
+
+
+def tile_list_twow_gatefetch_one_scattered_kernel(
+    tc, xt_words, xt_scales, w_words, w_scales, w2_words, w2_scales, sg, bg, wb_words, wb_scales, offs, offs2, offs3, offs4, out
+):
+    nc = tc.nc
+    with ExitStack() as ctx:
+        keep = ctx.enter_context(tc.tile_pool(name="keep", bufs=1))
+        psum = ctx.enter_context(tc.psum_pool(name="psum", bufs=1))
+
+        def sb(name, cols, dtype):
+            return keep.tile([P, cols], dtype, name=name, align_bytes=64)
+
+        l1 = sb("l1", J // 16, U16)
+        l2 = sb("l2", O // 16, U16)
+        l3 = sb("l3", O // 16, U16)
+        l4 = sb("l4", O // 16, U16)
+        xw = sb("xw", T, U32)
+        xs = sb("xs", T, U8)
+        ww = sb("ww", 2 * R, U8)
+        w2w = sb("w2w", R, U32)
+        wbw = sb("wbw", N, U32)
+        wsc = sb("wsc", 2 * R + N, U8)
+        ws, w2s, wbs = wsc[:, 0:R], wsc[:, R : 2 * R], wsc[:, 2 * R : 2 * R + N]
+        slope = sb("slope", PACK, F32)
+        shift = sb("shift", PACK, F32)
+        xg = sb("xg", J, U32)
+        xgs = sb("xgs", J, U8)
+        wwp = sb("wwp", 2 * R, U8)
+        w2wp = sb("w2wp", R, U32)
+        wsp = sb("wsp", R, U8)
+        w2sp = wsp
+        a_sb = [sb("a%d" % t, J, F32) for t in range(PACK)]
+        b_sb = [sb("b%d" % t, J, F32) for t in range(PACK)]
+        gate = sb("gate", PACK * O, F32)
+        picked = sb("picked", PACK * O, F32)
+        hid = sb("hid", PACK * O, BF16)
+        hq = sb("hq", O, U32)
+        hs = sb("hs", O, U8)
+        p_sb = [sb("p%d" % n, O, F32) for n in range(N // P)]
+        pages = [sb("page%d" % n, E, F32) for n in range(N // P)]
+
+        nc.vector.memset(wsc[:].bitcast(I32), 0)
+        for page in pages:
+            nc.vector.memset(page[:], 0.0)
+
+        def rows(q, plane, src, quad):
+            q.dma_start(out=plane[32 * quad : 32 * quad + 4, :].bitcast(I32), in_=src[0, 4 * quad : 4 * quad + 4, :].bitcast(I32))
+
+        def words(q, tile, src):
+            q.dma_start(out=tile[:].bitcast(I32), in_=src[0].rearrange("p n t -> p (n t)").bitcast(I32))
+
+        def per_row(q, tile, src):
+            q.dma_start(out=tile[:], in_=src.rearrange("(p t) o -> p (t o)", t=PACK))
+
+        S, A, G = nc.sync, nc.scalar, nc.gpsimd
+        S.dma_start(out=xs[0 : 32, :].bitcast(I32), in_=xt_scales[0, 0 : 4, :].bitcast(I32).unsqueeze(0).to_broadcast([8, 4, T // 4]))
+        A.dma_start(out=xs[32 : 64, :].bitcast(I32), in_=xt_scales[0, 4 : 8, :].bitcast(I32).unsqueeze(0).to_broadcast([8, 4, T // 4]))
+        S.dma_start(out=xs[64 : 96, :].bitcast(I32), in_=xt_scales[0, 8 : 12, :].bitcast(I32).unsqueeze(0).to_broadcast([8, 4, T // 4]))
+        A.dma_start(out=xs[96 : 128, :].bitcast(I32), in_=xt_scales[0, 12 : 16, :].bitcast(I32).unsqueeze(0).to_broadcast([8, 4, T // 4]))
+        S.dma_start(l1[:], offs)
+        words(A, xw, xt_words)
+        S.dma_start(out=ww[:].bitcast(I32), in_=w_words[0].bitcast(I32))
+        S.dma_start(l2[:], offs2)
+        rows(S, ws, w_scales, 0)
+        rows(S, ws, w_scales, 1)
+        words(A, w2w, w2_words)
+        rows(S, ws, w_scales, 2)
+        rows(S, ws, w_scales, 3)
+        per_row(S, slope, sg)
+        per_row(S, shift, bg)
+        rows(S, w2s, w2_scales, 0)
+        S.dma_start(l3[:], offs3)
+        words(S, wbw, wb_words)
+        rows(S, wbs, wb_scales, 0)
+        rows(S, wbs, wb_scales, 1)
+        rows(S, wbs, wb_scales, 2)
+        rows(S, wbs, wb_scales, 3)
+        S.dma_start(l4[:], offs4)
+        rows(G, w2s, w2_scales, 1)
+        rows(G, w2s, w2_scales, 2)
+        rows(G, w2s, w2_scales, 3)
+
+        def deal(dst, src):
+            nc.vector.tensor_copy(out=dst.rearrange("p (t m) -> p t m", t=PACK), in_=src.rearrange("p (m t) -> p t m", t=PACK))
+
+        banks = {}
+
+        def mm_a(t):
+            banks["a", t] = psum.tile([P, J], F32, name="bank%d" % t)
+            nc.tensor.matmul_mx(out=banks["a", t][:], lhsT=wwp[:, 2 * P * t : 2 * P * (t + 1)].bitcast(E2M1), lhsT_scale=wsp[:, P * t : P * (t + 1)],
+                                rhs=xg[:].bitcast(E4M3), rhs_scale=xgs[:], start=True, stop=True)
+
+        def mm_b(t):
+            banks["b", t] = psum.tile([P, J], F32, name="bank%d" % (PACK + t))
+            nc.tensor.matmul_mx(out=banks["b", t][:], lhsT=w2wp[:, P * t : P * (t + 1)].bitcast(E5M2), lhsT_scale=w2sp[:, P * t : P * (t + 1)],
+                                rhs=xg[:].bitcast(E4M3), rhs_scale=xgs[:], start=True, stop=True)
+
+        def copy(on_vector, dst, src):
+            if on_vector:
+                nc.vector.tensor_copy(out=dst, in_=src)
+            else:
+                nc.scalar.copy(out=dst, in_=src)
+
+        def ea(t, v):
+            copy(v, a_sb[t][:], banks["a", t][:])
+
+        def eb(t, v):
+            copy(v, b_sb[t][:], banks["b", t][:])
+
+        def sig(t):
+            nc.scalar.activation(out=gate[:, O * t : O * (t + 1)], in_=a_sb[t][:].indirect(l2[:]), func=ACT.Sigmoid,
+                                 bias=shift[:, t : t + 1], scale=slope[:, t : t + 1])
+
+        def gb(t, v):
+            if v:
+                nc.vector.tensor_copy(out=picked[:, O * t : O * (t + 1)], in_=b_sb[t][:].indirect(l3[:]))
+            else:
+                nc.scalar.activation(out=picked[:, O * t : O * (t + 1)], in_=b_sb[t][:].indirect(l3[:]), func=ACT.Copy)
+
+        nc.vector.tensor_copy(out=xgs[:], in_=xs[:].indirect(l1[:]))
+        deal(wwp[:].bitcast(U16), ww[:].bitcast(U16))
+        nc.vector.tensor_copy(out=xg[:], in_=xw[:].indirect(l1[:]))
+        nc.vector.tensor_copy(out=wsp[:, 0 : 256].rearrange("p (t m) -> p t m", t=2), in_=ws.rearrange("p (m t) -> p t m", t=PACK)[:, 0 : 2, :])
+        nc.vector.tensor_copy(out=wsp[:, 256 : 512].rearrange("p (t m) -> p t m", t=2), in_=ws.rearrange("p (m t) -> p t m", t=PACK)[:, 2 : 4, :])
+        deal(w2wp[:], w2w[:])
+        for t in range(PACK):
+            mm_a(t)
+            ea(t, t % 2 == 0)
+        for t in range(PACK):
+            sig(t)
+        nc.vector.tensor_copy(out=w2sp[:, 0 : 256].rearrange("p (t m) -> p t m", t=2), in_=w2s.rearrange("p (m t) -> p t m", t=PACK)[:, 0 : 2, :])
+        nc.vector.tensor_copy(out=w2sp[:, 256 : 512].rearrange("p (t m) -> p t m", t=2), in_=w2s.rearrange("p (m t) -> p t m", t=PACK)[:, 2 : 4, :])
+        for t in range(PACK):
+            mm_b(t)
+            eb(t, t != 3)
+        for t in range(PACK):
+            gb(t, t != 3)
+
+        H = O // 2
+        for h in range(2):
+            nc.vector.tensor_tensor(out=hid[:, PACK * H * h : PACK * H * (h + 1)].rearrange("p (c i t) -> p c t i", i=4, t=PACK),
+                                    in0=picked[:].rearrange("p (t c i) -> p c t i", i=4, t=PACK)[:, H // 4 * h : H // 4 * (h + 1)],
+                                    in1=gate[:].rearrange("p (t c i) -> p c t i", i=4, t=PACK)[:, H // 4 * h : H // 4 * (h + 1)], op=MULT)
+        for h in range(2):
+            nc.vector.quantize_mx(out=hq[:, H * h : H * (h + 1)].bitcast(E4M3), scales=hs[:, H * h : H * (h + 1)], in_=hid[:, PACK * H * h : PACK * H * (h + 1)])
+        for n in range(N // P):
+            bank = psum.tile([P, O], F32, name="bank%d" % n)
+            nc.tensor.matmul_mx(out=bank[:], lhsT=wbw[:, P * n : P * (n + 1)].bitcast(E5M2), lhsT_scale=wbs[:, P * n : P * (n + 1)],
+                                rhs=hq[:].bitcast(E4M3), rhs_scale=hs[:], start=True, stop=True)
+            copy(n == 1, p_sb[n][:], bank[:])
+        nc.scalar.activation(out=pages[0][:].indirect(l4[:]), in_=p_sb[0][:], func=ACT.Copy)
+        nc.vector.tensor_copy(out=pages[1][:].indirect(l4[:]), in_=p_sb[1][:])
+        A.dma_start(out=out[0:P, :], in_=pages[0][:])
+        S.dma_start(out=out[P : 2 * P, :], in_=pages[1][:])

@@ -61,6 +61,9 @@ def tile_list_twow_gatefetch_one_scattered_kernel(
         pages = [sb("page%d" % n, E, F32) for n in range(N // P)]
 
         nc.vector.memset(wsc[:].bitcast(I32), 0)
+        warm_in = sb("warm_in", 16, F32)
+        warm_out = sb("warm_out", 16, F32)
+        nc.vector.memset(warm_in[:, 0:1], 0.0)
         for page in pages:
             nc.vector.memset(page[:], 0.0)
 
@@ -100,6 +103,7 @@ def tile_list_twow_gatefetch_one_scattered_kernel(
         rows(G, w2s, w2_scales, 1)
         rows(G, w2s, w2_scales, 2)
         rows(G, w2s, w2_scales, 3)
+        nc.scalar.activation(out=warm_out[:, 0:1], in_=warm_in[:, 0:1], func=ACT.Sigmoid)
 
         def deal(dst, src):
             nc.vector.tensor_copy(out=dst.rearrange("p (t m) -> p t m", t=PACK), in_=src.rearrange("p (m t) -> p t m", t=PACK))

@@ -49,7 +49,7 @@ def tile_list_twow_gatefetch_one_scattered_kernel(
         wwp = sb("wwp", 2 * R, U8)
         w2wp = sb("w2wp", R, U32)
         wsp = sb("wsp", R, U8)
-        w2sp = wsp
+        w2sp = sb("w2sp", R, U8)
         a_sb = [sb("a%d" % t, J, F32) for t in range(PACK)]
         b_sb = [sb("b%d" % t, J, F32) for t in range(PACK)]
         gate = sb("gate", PACK * O, F32)
@@ -60,7 +60,8 @@ def tile_list_twow_gatefetch_one_scattered_kernel(
         p_sb = [sb("p%d" % n, O, F32) for n in range(N // P)]
         pages = [sb("page%d" % n, E, F32) for n in range(N // P)]
 
-        nc.vector.memset(wsc[:].bitcast(I32), 0)
+        nc.vector.memset(wsc[:, 0:R].bitcast(I32), 0)
+        nc.vector.memset(wsc[:, R:].bitcast(I32), 0)
         warm_in = sb("warm_in", 16, F32)
         warm_out = sb("warm_out", 16, F32)
         nc.vector.memset(warm_in[:, 0:1], 0.0)
@@ -83,26 +84,26 @@ def tile_list_twow_gatefetch_one_scattered_kernel(
         A.dma_start(out=xs[96 : 128, :].bitcast(I32), in_=xt_scales[0, 12 : 16, :].bitcast(I32).unsqueeze(0).to_broadcast([8, 4, T // 4]))
         S.dma_start(l1[:], offs)
         words(A, xw, xt_words)
+        words(S, w2w, w2_words)
         S.dma_start(out=ww[:].bitcast(I32), in_=w_words[0].bitcast(I32))
-        S.dma_start(l2[:], offs2)
+        rows(S, w2s, w2_scales, 0)
+        rows(A, w2s, w2_scales, 1)
+        rows(S, w2s, w2_scales, 2)
+        rows(A, w2s, w2_scales, 3)
         rows(S, ws, w_scales, 0)
         rows(S, ws, w_scales, 1)
-        words(A, w2w, w2_words)
-        rows(S, ws, w_scales, 2)
-        rows(S, ws, w_scales, 3)
+        S.dma_start(l3[:], offs3)
+        S.dma_start(l2[:], offs2)
         per_row(S, slope, sg)
         per_row(S, shift, bg)
-        rows(S, w2s, w2_scales, 0)
-        S.dma_start(l3[:], offs3)
         words(S, wbw, wb_words)
         rows(S, wbs, wb_scales, 0)
         rows(S, wbs, wb_scales, 1)
         rows(S, wbs, wb_scales, 2)
         rows(S, wbs, wb_scales, 3)
         S.dma_start(l4[:], offs4)
-        rows(G, w2s, w2_scales, 1)
-        rows(G, w2s, w2_scales, 2)
-        rows(G, w2s, w2_scales, 3)
+        rows(G, ws, w_scales, 2)
+        rows(G, ws, w_scales, 3)
         nc.scalar.activation(out=warm_out[:, 0:1], in_=warm_in[:, 0:1], func=ACT.Sigmoid)
 
         def deal(dst, src):
@@ -136,6 +137,11 @@ def tile_list_twow_gatefetch_one_scattered_kernel(
             nc.scalar.activation(out=gate[:, O * t : O * (t + 1)], in_=a_sb[t][:].indirect(l2[:]), func=ACT.Sigmoid,
                                  bias=shift[:, t : t + 1], scale=slope[:, t : t + 1])
 
+        def mul(u, c0, c1):
+            nc.vector.tensor_tensor(out=hid[:].rearrange("p (c i u v) -> p u c v i", i=4, u=2, v=2)[:, u, c0:c1],
+                                    in0=picked[:].rearrange("p (u v c i) -> p u c v i", i=4, u=2, v=2)[:, u, c0:c1],
+                                    in1=gate[:].rearrange("p (u v c i) -> p u c v i", i=4, u=2, v=2)[:, u, c0:c1], op=MULT)
+
         def gb(t, v):
             if v:
                 nc.vector.tensor_copy(out=picked[:, O * t : O * (t + 1)], in_=b_sb[t][:].indirect(l3[:]))
@@ -143,31 +149,41 @@ def tile_list_twow_gatefetch_one_scattered_kernel(
                 nc.scalar.activation(out=picked[:, O * t : O * (t + 1)], in_=b_sb[t][:].indirect(l3[:]), func=ACT.Copy)
 
         nc.vector.tensor_copy(out=xgs[:], in_=xs[:].indirect(l1[:]))
-        deal(wwp[:].bitcast(U16), ww[:].bitcast(U16))
         nc.vector.tensor_copy(out=xg[:], in_=xw[:].indirect(l1[:]))
+        nc.vector.tensor_copy(out=w2wp[:, 0 : 256].rearrange("p (t m) -> p t m", t=2), in_=w2w[:].rearrange("p (m t) -> p t m", t=PACK)[:, 0 : 2, :])
+        nc.scalar.copy(out=w2wp[:, 256 : 512].rearrange("p (t m) -> p t m", t=2), in_=w2w[:].rearrange("p (m t) -> p t m", t=PACK)[:, 2 : 4, :])
+        nc.scalar.copy(out=wwp[:].bitcast(U16).rearrange("p (t m) -> p t m", t=PACK), in_=ww[:].bitcast(U16).rearrange("p (m t) -> p t m", t=PACK))
+        nc.vector.tensor_copy(out=w2sp[:, 0 : 128], in_=w2s.rearrange("p (m t) -> p t m", t=PACK)[:, 0, :])
+        nc.vector.tensor_copy(out=w2sp[:, 128 : 256], in_=w2s.rearrange("p (m t) -> p t m", t=PACK)[:, 1, :])
+        nc.vector.tensor_copy(out=w2sp[:, 256 : 384], in_=w2s.rearrange("p (m t) -> p t m", t=PACK)[:, 2, :])
+        nc.vector.tensor_copy(out=w2sp[:, 384 : 512], in_=w2s.rearrange("p (m t) -> p t m", t=PACK)[:, 3, :])
         nc.vector.tensor_copy(out=wsp[:, 0 : 256].rearrange("p (t m) -> p t m", t=2), in_=ws.rearrange("p (m t) -> p t m", t=PACK)[:, 0 : 2, :])
         nc.vector.tensor_copy(out=wsp[:, 256 : 512].rearrange("p (t m) -> p t m", t=2), in_=ws.rearrange("p (m t) -> p t m", t=PACK)[:, 2 : 4, :])
-        deal(w2wp[:], w2w[:])
-        for t in range(PACK):
-            mm_a(t)
-            ea(t, t % 2 == 0)
-        for t in range(PACK):
-            sig(t)
-        nc.vector.tensor_copy(out=w2sp[:, 0 : 256].rearrange("p (t m) -> p t m", t=2), in_=w2s.rearrange("p (m t) -> p t m", t=PACK)[:, 0 : 2, :])
-        nc.vector.tensor_copy(out=w2sp[:, 256 : 512].rearrange("p (t m) -> p t m", t=2), in_=w2s.rearrange("p (m t) -> p t m", t=PACK)[:, 2 : 4, :])
         for t in range(PACK):
             mm_b(t)
-            eb(t, t != 3)
+            eb(t, False)
         for t in range(PACK):
-            gb(t, t != 3)
+            mm_a(t)
+            ea(t, True)
+            if t < PACK - 1:
+                sig(t)
+        gb(0, True)
+        gb(1, True)
+        gb(2, False)
+        gb(3, False)
+        mul(0, 0, 32)
+        for h in range(2):
+            nc.scalar.activation(out=gate[:, O * 3 + 64 * h : O * 3 + 64 * (h + 1)], in_=a_sb[3][:].indirect(l2[:, 4 * h : 4 * h + 4]), func=ACT.Sigmoid, bias=shift[:, 3:4], scale=slope[:, 3:4])
+        for h in range(2):
+            mul(1, 16 * h, 16 * h + 16)
+        for h in range(2):
+            nc.vector.quantize_mx(out=hq[:, 64 * h : 64 * h + 64].bitcast(E4M3), scales=hs[:, 64 * h : 64 * h + 64], in_=hid[:, 256 * h : 256 * h + 256])
 
-        H = O // 2
-        for h in range(2):
-            nc.vector.tensor_tensor(out=hid[:, PACK * H * h : PACK * H * (h + 1)].rearrange("p (c i t) -> p c t i", i=4, t=PACK),
-                                    in0=picked[:].rearrange("p (t c i) -> p c t i", i=4, t=PACK)[:, H // 4 * h : H // 4 * (h + 1)],
-                                    in1=gate[:].rearrange("p (t c i) -> p c t i", i=4, t=PACK)[:, H // 4 * h : H // 4 * (h + 1)], op=MULT)
-        for h in range(2):
-            nc.vector.quantize_mx(out=hq[:, H * h : H * (h + 1)].bitcast(E4M3), scales=hs[:, H * h : H * (h + 1)], in_=hid[:, PACK * H * h : PACK * H * (h + 1)])
+        nc.vector.quantize_mx(out=hq[:, 64 * h : 64 * h + 64].bitcast(E4M3), scales=hs[:, 64 * h : 64 * h + 64], in_=hid[:, 256 * h : 256 * h + 256])
+
+        nc.vector.tensor_tensor(out=hid[:].rearrange("p (c i t) -> p c t i", i=4, t=PACK),
+                                in0=picked[:].rearrange("p (t c i) -> p c t i", i=4, t=PACK),
+                                in1=gate[:].rearrange("p (t c i) -> p c t i", i=4, t=PACK), op=MULT)
         for n in range(N // P):
             bank = psum.tile([P, O], F32, name="bank%d" % n)
             nc.tensor.matmul_mx(out=bank[:], lhsT=wbw[:, P * n : P * (n + 1)].bitcast(E5M2), lhsT_scale=wbs[:, P * n : P * (n + 1)],

@@ -3,7 +3,7 @@ from contextlib import ExitStack
 import concourse.mybir as mybir
 
 K, T, J, R, O, N, E = 512, 1024, 256, 512, 128, 256, 1024
-FLOPS = 2 * K * R * J * 2 + 2 * R * N * O
+FLOPS = 2 * (2 * K * R * J) + 2 * R * N * O
 
 F32 = mybir.dt.float32
 BF16 = mybir.dt.bfloat16
@@ -16,8 +16,15 @@ E5M2 = mybir.dt.float8_e5m2_x4
 E2M1 = mybir.dt.float4_e2m1fn_x4
 ACT = mybir.ActivationFunctionType
 MULT = mybir.AluOpType.mult
+
 P = 128
 PACK = 4
+QUADS = 4
+QUAD = P // QUADS
+LIVE = 4
+GROUP = 16
+LINE = 4
+HALF = O // 2
 
 
 def tile_list_twow_gatefetch_one_scattered_kernel(
@@ -28,168 +35,171 @@ def tile_list_twow_gatefetch_one_scattered_kernel(
         keep = ctx.enter_context(tc.tile_pool(name="keep", bufs=1))
         psum = ctx.enter_context(tc.psum_pool(name="psum", bufs=1))
 
-        def sb(name, cols, dtype):
+        def sbuf(name, cols, dtype):
             return keep.tile([P, cols], dtype, name=name, align_bytes=64)
 
-        l1 = sb("l1", J // 16, U16)
-        l2 = sb("l2", O // 16, U16)
-        l3 = sb("l3", O // 16, U16)
-        l4 = sb("l4", O // 16, U16)
-        xw = sb("xw", T, U32)
-        xs = sb("xs", T, U8)
-        ww = sb("ww", 2 * R, U8)
-        w2w = sb("w2w", R, U32)
-        wbw = sb("wbw", N, U32)
-        wsc = sb("wsc", 2 * R + N, U8)
-        ws, w2s, wbs = wsc[:, 0:R], wsc[:, R : 2 * R], wsc[:, 2 * R : 2 * R + N]
-        slope = sb("slope", PACK, F32)
-        shift = sb("shift", PACK, F32)
-        xg = sb("xg", J, U32)
-        xgs = sb("xgs", J, U8)
-        wwp = sb("wwp", 2 * R, U8)
-        w2wp = sb("w2wp", R, U32)
-        wsp = sb("wsp", R, U8)
-        w2sp = sb("w2sp", R, U8)
-        a_sb = [sb("a%d" % t, J, F32) for t in range(PACK)]
-        b_sb = [sb("b%d" % t, J, F32) for t in range(PACK)]
-        gate = sb("gate", PACK * O, F32)
-        picked = sb("picked", PACK * O, F32)
-        hid = sb("hid", PACK * O, BF16)
-        hq = sb("hq", O, U32)
-        hs = sb("hs", O, U8)
-        p_sb = [sb("p%d" % n, O, F32) for n in range(N // P)]
-        pages = [sb("page%d" % n, E, F32) for n in range(N // P)]
+        tokens = sbuf("tokens", J // GROUP, U16)
+        gate_slots = sbuf("gate_slots", O // GROUP, U16)
+        value_slots = sbuf("value_slots", O // GROUP, U16)
+        page_cols = sbuf("page_cols", O // GROUP, U16)
+        x_words = sbuf("x_words", T, U32)
+        x_plane = sbuf("x_plane", T, U8)
+        w_raw = sbuf("w_raw", 2 * R, U8)
+        w2_raw = sbuf("w2_raw", R, U32)
+        wb_codes = sbuf("wb_codes", N, U32)
+        planes = sbuf("planes", 2 * R + N, U8)
+        w_plane, w2_plane, wb_plane = planes[:, 0:R], planes[:, R : 2 * R], planes[:, 2 * R :]
+        slope = sbuf("slope", PACK, F32)
+        shift = sbuf("shift", PACK, F32)
+        xg_words = sbuf("xg_words", J, U32)
+        xg_plane = sbuf("xg_plane", J, U8)
+        w_dealt = sbuf("w_dealt", 2 * R, U8)
+        w2_dealt = sbuf("w2_dealt", R, U32)
+        w_plane_dealt = sbuf("w_plane_dealt", R, U8)
+        w2_plane_dealt = sbuf("w2_plane_dealt", R, U8)
+        a_slices = [sbuf("a%d" % t, J, F32) for t in range(PACK)]
+        b_slices = [sbuf("b%d" % t, J, F32) for t in range(PACK)]
+        gate = sbuf("gate", PACK * O, F32)
+        value = sbuf("value", PACK * O, F32)
+        hid = sbuf("hid", PACK * O, BF16)
+        hid_words = sbuf("hid_words", O, U32)
+        hid_plane = sbuf("hid_plane", O, U8)
+        p_tiles = [sbuf("p%d" % n, O, F32) for n in range(N // P)]
+        pages = [sbuf("page%d" % n, E, F32) for n in range(N // P)]
+        warm_in = sbuf("warm_in", 16, F32)
+        warm_out = sbuf("warm_out", 16, F32)
 
-        nc.vector.memset(wsc[:, 0:R].bitcast(I32), 0)
-        nc.vector.memset(wsc[:, R:].bitcast(I32), 0)
-        warm_in = sb("warm_in", 16, F32)
-        warm_out = sb("warm_out", 16, F32)
+        nc.vector.memset(w_plane.bitcast(I32), 0)
+        nc.vector.memset(planes[:, R:].bitcast(I32), 0)
         nc.vector.memset(warm_in[:, 0:1], 0.0)
         for page in pages:
             nc.vector.memset(page[:], 0.0)
 
-        def rows(q, plane, src, quad):
-            q.dma_start(out=plane[32 * quad : 32 * quad + 4, :].bitcast(I32), in_=src[0, 4 * quad : 4 * quad + 4, :].bitcast(I32))
+        def load_rows(queue, plane, scales, q):
+            queue.dma_start(
+                out=plane[QUAD * q : QUAD * q + LIVE, :].bitcast(I32), in_=scales[0, LIVE * q : LIVE * (q + 1), :].bitcast(I32)
+            )
 
-        def words(q, tile, src):
-            q.dma_start(out=tile[:].bitcast(I32), in_=src[0].rearrange("p n t -> p (n t)").bitcast(I32))
+        def load_x_rows(queue, q):
+            rows = xt_scales[0, LIVE * q : LIVE * (q + 1), :].bitcast(I32)
+            queue.dma_start(
+                out=x_plane[QUAD * q : QUAD * (q + 1), :].bitcast(I32),
+                in_=rows.unsqueeze(0).to_broadcast([QUAD // LIVE, LIVE, T // 4]),
+            )
 
-        def per_row(q, tile, src):
-            q.dma_start(out=tile[:], in_=src.rearrange("(p t) o -> p (t o)", t=PACK))
+        def load_words(queue, tile, words):
+            queue.dma_start(out=tile[:].bitcast(I32), in_=words[0].rearrange("p n t -> p (n t)").bitcast(I32))
 
-        S, A, G = nc.sync, nc.scalar, nc.gpsimd
-        S.dma_start(out=xs[0 : 32, :].bitcast(I32), in_=xt_scales[0, 0 : 4, :].bitcast(I32).unsqueeze(0).to_broadcast([8, 4, T // 4]))
-        A.dma_start(out=xs[32 : 64, :].bitcast(I32), in_=xt_scales[0, 4 : 8, :].bitcast(I32).unsqueeze(0).to_broadcast([8, 4, T // 4]))
-        S.dma_start(out=xs[64 : 96, :].bitcast(I32), in_=xt_scales[0, 8 : 12, :].bitcast(I32).unsqueeze(0).to_broadcast([8, 4, T // 4]))
-        A.dma_start(out=xs[96 : 128, :].bitcast(I32), in_=xt_scales[0, 12 : 16, :].bitcast(I32).unsqueeze(0).to_broadcast([8, 4, T // 4]))
-        S.dma_start(l1[:], offs)
-        words(A, xw, xt_words)
-        words(S, w2w, w2_words)
-        S.dma_start(out=ww[:].bitcast(I32), in_=w_words[0].bitcast(I32))
-        rows(S, w2s, w2_scales, 0)
-        rows(A, w2s, w2_scales, 1)
-        rows(S, w2s, w2_scales, 2)
-        rows(A, w2s, w2_scales, 3)
-        rows(S, ws, w_scales, 0)
-        rows(S, ws, w_scales, 1)
-        S.dma_start(l3[:], offs3)
-        S.dma_start(l2[:], offs2)
-        per_row(S, slope, sg)
-        per_row(S, shift, bg)
-        words(S, wbw, wb_words)
-        rows(S, wbs, wb_scales, 0)
-        rows(S, wbs, wb_scales, 1)
-        rows(S, wbs, wb_scales, 2)
-        rows(S, wbs, wb_scales, 3)
-        S.dma_start(l4[:], offs4)
-        rows(G, ws, w_scales, 2)
-        rows(G, ws, w_scales, 3)
+        def load_by_slice(tile, column):
+            nc.sync.dma_start(out=tile[:], in_=column.rearrange("(p t) o -> p (t o)", t=PACK))
+
+        both_queues = (nc.sync, nc.scalar)
+        for q in range(QUADS):
+            load_x_rows(both_queues[q % 2], q)
+        nc.sync.dma_start(tokens[:], offs)
+        load_words(nc.scalar, x_words, xt_words)
+        load_words(nc.sync, w2_raw, w2_words)
+        nc.sync.dma_start(out=w_raw[:].bitcast(I32), in_=w_words[0].bitcast(I32))
+        for q in range(QUADS):
+            load_rows(both_queues[q % 2], w2_plane, w2_scales, q)
+        for q in range(QUADS // 2):
+            load_rows(nc.sync, w_plane, w_scales, q)
+        nc.sync.dma_start(value_slots[:], offs3)
+        nc.sync.dma_start(gate_slots[:], offs2)
+        load_by_slice(slope, sg)
+        load_by_slice(shift, bg)
+        load_words(nc.sync, wb_codes, wb_words)
+        for q in range(QUADS):
+            load_rows(nc.sync, wb_plane, wb_scales, q)
+        nc.sync.dma_start(page_cols[:], offs4)
+        for q in range(QUADS // 2, QUADS):
+            load_rows(nc.gpsimd, w_plane, w_scales, q)
+
         nc.scalar.activation(out=warm_out[:, 0:1], in_=warm_in[:, 0:1], func=ACT.Sigmoid)
 
-        def deal(dst, src):
-            nc.vector.tensor_copy(out=dst.rearrange("p (t m) -> p t m", t=PACK), in_=src.rearrange("p (m t) -> p t m", t=PACK))
+        def deal(copy, dealt, raw, first, count):
+            slices = slice(first, first + count)
+            copy(out=dealt.rearrange("p (t m) -> p t m", t=PACK)[:, slices, :], in_=raw.rearrange("p (m t) -> p t m", t=PACK)[:, slices, :])
 
-        banks = {}
+        nc.vector.tensor_copy(out=xg_plane[:], in_=x_plane[:].indirect(tokens[:]))
+        nc.vector.tensor_copy(out=xg_words[:], in_=x_words[:].indirect(tokens[:]))
 
-        def mm_a(t):
-            banks["a", t] = psum.tile([P, J], F32, name="bank%d" % t)
-            nc.tensor.matmul_mx(out=banks["a", t][:], lhsT=wwp[:, 2 * P * t : 2 * P * (t + 1)].bitcast(E2M1), lhsT_scale=wsp[:, P * t : P * (t + 1)],
-                                rhs=xg[:].bitcast(E4M3), rhs_scale=xgs[:], start=True, stop=True)
-
-        def mm_b(t):
-            banks["b", t] = psum.tile([P, J], F32, name="bank%d" % (PACK + t))
-            nc.tensor.matmul_mx(out=banks["b", t][:], lhsT=w2wp[:, P * t : P * (t + 1)].bitcast(E5M2), lhsT_scale=w2sp[:, P * t : P * (t + 1)],
-                                rhs=xg[:].bitcast(E4M3), rhs_scale=xgs[:], start=True, stop=True)
-
-        def copy(on_vector, dst, src):
-            if on_vector:
-                nc.vector.tensor_copy(out=dst, in_=src)
-            else:
-                nc.scalar.copy(out=dst, in_=src)
-
-        def ea(t, v):
-            copy(v, a_sb[t][:], banks["a", t][:])
-
-        def eb(t, v):
-            copy(v, b_sb[t][:], banks["b", t][:])
-
-        def sig(t):
-            nc.scalar.activation(out=gate[:, O * t : O * (t + 1)], in_=a_sb[t][:].indirect(l2[:]), func=ACT.Sigmoid,
-                                 bias=shift[:, t : t + 1], scale=slope[:, t : t + 1])
-
-        def mul(u, c0, c1):
-            nc.vector.tensor_tensor(out=hid[:].rearrange("p (c i u v) -> p u c v i", i=4, u=2, v=2)[:, u, c0:c1],
-                                    in0=picked[:].rearrange("p (u v c i) -> p u c v i", i=4, u=2, v=2)[:, u, c0:c1],
-                                    in1=gate[:].rearrange("p (u v c i) -> p u c v i", i=4, u=2, v=2)[:, u, c0:c1], op=MULT)
-
-        def gb(t, v):
-            if v:
-                nc.vector.tensor_copy(out=picked[:, O * t : O * (t + 1)], in_=b_sb[t][:].indirect(l3[:]))
-            else:
-                nc.scalar.activation(out=picked[:, O * t : O * (t + 1)], in_=b_sb[t][:].indirect(l3[:]), func=ACT.Copy)
-
-        nc.vector.tensor_copy(out=xgs[:], in_=xs[:].indirect(l1[:]))
-        nc.vector.tensor_copy(out=xg[:], in_=xw[:].indirect(l1[:]))
-        nc.vector.tensor_copy(out=w2wp[:, 0 : 256].rearrange("p (t m) -> p t m", t=2), in_=w2w[:].rearrange("p (m t) -> p t m", t=PACK)[:, 0 : 2, :])
-        nc.scalar.copy(out=w2wp[:, 256 : 512].rearrange("p (t m) -> p t m", t=2), in_=w2w[:].rearrange("p (m t) -> p t m", t=PACK)[:, 2 : 4, :])
-        nc.scalar.copy(out=wwp[:].bitcast(U16).rearrange("p (t m) -> p t m", t=PACK), in_=ww[:].bitcast(U16).rearrange("p (m t) -> p t m", t=PACK))
-        nc.vector.tensor_copy(out=w2sp[:, 0 : 128], in_=w2s.rearrange("p (m t) -> p t m", t=PACK)[:, 0, :])
-        nc.vector.tensor_copy(out=w2sp[:, 128 : 256], in_=w2s.rearrange("p (m t) -> p t m", t=PACK)[:, 1, :])
-        nc.vector.tensor_copy(out=w2sp[:, 256 : 384], in_=w2s.rearrange("p (m t) -> p t m", t=PACK)[:, 2, :])
-        nc.vector.tensor_copy(out=w2sp[:, 384 : 512], in_=w2s.rearrange("p (m t) -> p t m", t=PACK)[:, 3, :])
-        nc.vector.tensor_copy(out=wsp[:, 0 : 256].rearrange("p (t m) -> p t m", t=2), in_=ws.rearrange("p (m t) -> p t m", t=PACK)[:, 0 : 2, :])
-        nc.vector.tensor_copy(out=wsp[:, 256 : 512].rearrange("p (t m) -> p t m", t=2), in_=ws.rearrange("p (m t) -> p t m", t=PACK)[:, 2 : 4, :])
+        deal(nc.vector.tensor_copy, w2_dealt[:], w2_raw[:], 0, PACK // 2)
+        deal(nc.scalar.copy, w2_dealt[:], w2_raw[:], PACK // 2, PACK // 2)
+        deal(nc.scalar.copy, w_dealt[:].bitcast(U16), w_raw[:].bitcast(U16), 0, PACK)
         for t in range(PACK):
-            mm_b(t)
-            eb(t, False)
+            deal(nc.vector.tensor_copy, w2_plane_dealt[:], w2_plane, t, 1)
+        for first in range(0, PACK, PACK // 2):
+            deal(nc.vector.tensor_copy, w_plane_dealt[:], w_plane, first, PACK // 2)
+
+        def first_product(bank_number, codes, plane):
+            bank = psum.tile([P, J], F32, name="bank%d" % bank_number)
+            nc.tensor.matmul_mx(
+                out=bank[:], lhsT=codes, lhsT_scale=plane, rhs=xg_words[:].bitcast(E4M3), rhs_scale=xg_plane[:], start=True, stop=True
+            )
+            return bank
+
+        def fetch_gate(t, first, count):
+            nc.scalar.activation(
+                out=gate[:, O * t + first : O * t + first + count],
+                in_=a_slices[t][:].indirect(gate_slots[:, first // GROUP : (first + count) // GROUP]),
+                func=ACT.Sigmoid,
+                bias=shift[:, t : t + 1],
+                scale=slope[:, t : t + 1],
+            )
+
+        def multiply(pair, first, count):
+            lines = slice(first // LINE, (first + count) // LINE)
+            by_slice = "p (u v c i) -> p u c v i"
+            nc.vector.tensor_tensor(
+                out=hid[:].rearrange("p (c i u v) -> p u c v i", i=LINE, u=2, v=2)[:, pair, lines],
+                in0=value[:].rearrange(by_slice, i=LINE, u=2, v=2)[:, pair, lines],
+                in1=gate[:].rearrange(by_slice, i=LINE, u=2, v=2)[:, pair, lines],
+                op=MULT,
+            )
+
+        last = PACK - 1
         for t in range(PACK):
-            mm_a(t)
-            ea(t, True)
-            if t < PACK - 1:
-                sig(t)
-        gb(0, True)
-        gb(1, True)
-        gb(2, False)
-        gb(3, False)
-        mul(0, 0, 32)
-        for h in range(2):
-            nc.scalar.activation(out=gate[:, O * 3 + 64 * h : O * 3 + 64 * (h + 1)], in_=a_sb[3][:].indirect(l2[:, 4 * h : 4 * h + 4]), func=ACT.Sigmoid, bias=shift[:, 3:4], scale=slope[:, 3:4])
-        for h in range(2):
-            mul(1, 16 * h, 16 * h + 16)
-        for h in range(2):
-            nc.vector.quantize_mx(out=hq[:, 64 * h : 64 * h + 64].bitcast(E4M3), scales=hs[:, 64 * h : 64 * h + 64], in_=hid[:, 256 * h : 256 * h + 256])
+            places = slice(P * t, P * (t + 1))
+            bank = first_product(PACK + t, w2_dealt[:, places].bitcast(E5M2), w2_plane_dealt[:, places])
+            nc.scalar.copy(out=b_slices[t][:], in_=bank[:])
+        for t in range(PACK):
+            bank = first_product(t, w_dealt[:, 2 * P * t : 2 * P * (t + 1)].bitcast(E2M1), w_plane_dealt[:, P * t : P * (t + 1)])
+            nc.vector.tensor_copy(out=a_slices[t][:], in_=bank[:])
+            if t < last:
+                fetch_gate(t, 0, O)
+        for t in range(PACK // 2):
+            nc.vector.tensor_copy(out=value[:, O * t : O * (t + 1)], in_=b_slices[t][:].indirect(value_slots[:]))
+        for t in range(PACK // 2, PACK):
+            nc.scalar.activation(out=value[:, O * t : O * (t + 1)], in_=b_slices[t][:].indirect(value_slots[:]), func=ACT.Copy)
+        multiply(0, 0, O)
 
-        nc.vector.quantize_mx(out=hq[:, 64 * h : 64 * h + 64].bitcast(E4M3), scales=hs[:, 64 * h : 64 * h + 64], in_=hid[:, 256 * h : 256 * h + 256])
+        halves = range(0, O, HALF)
+        for first in halves:
+            fetch_gate(last, first, HALF)
+        for first in halves:
+            multiply(1, first, HALF)
+        for first in halves:
+            nc.vector.quantize_mx(
+                out=hid_words[:, first : first + HALF].bitcast(E4M3),
+                scales=hid_plane[:, first : first + HALF],
+                in_=hid[:, PACK * first : PACK * (first + HALF)],
+            )
 
-        nc.vector.tensor_tensor(out=hid[:].rearrange("p (c i t) -> p c t i", i=4, t=PACK),
-                                in0=picked[:].rearrange("p (t c i) -> p c t i", i=4, t=PACK),
-                                in1=gate[:].rearrange("p (t c i) -> p c t i", i=4, t=PACK), op=MULT)
-        for n in range(N // P):
+        for n, copy_out in enumerate((nc.scalar.copy, nc.vector.tensor_copy)):
+            features = slice(P * n, P * (n + 1))
             bank = psum.tile([P, O], F32, name="bank%d" % n)
-            nc.tensor.matmul_mx(out=bank[:], lhsT=wbw[:, P * n : P * (n + 1)].bitcast(E5M2), lhsT_scale=wbs[:, P * n : P * (n + 1)],
-                                rhs=hq[:].bitcast(E4M3), rhs_scale=hs[:], start=True, stop=True)
-            copy(n == 1, p_sb[n][:], bank[:])
-        nc.scalar.activation(out=pages[0][:].indirect(l4[:]), in_=p_sb[0][:], func=ACT.Copy)
-        nc.vector.tensor_copy(out=pages[1][:].indirect(l4[:]), in_=p_sb[1][:])
-        A.dma_start(out=out[0:P, :], in_=pages[0][:])
-        S.dma_start(out=out[P : 2 * P, :], in_=pages[1][:])
+            nc.tensor.matmul_mx(
+                out=bank[:],
+                lhsT=wb_codes[:, features].bitcast(E5M2),
+                lhsT_scale=wb_plane[:, features],
+                rhs=hid_words[:].bitcast(E4M3),
+                rhs_scale=hid_plane[:],
+                start=True,
+                stop=True,
+            )
+            copy_out(out=p_tiles[n][:], in_=bank[:])
+        nc.scalar.activation(out=pages[0][:].indirect(page_cols[:]), in_=p_tiles[0][:], func=ACT.Copy)
+        nc.vector.tensor_copy(out=pages[1][:].indirect(page_cols[:]), in_=p_tiles[1][:])
+        nc.scalar.dma_start(out=out[0:P, :], in_=pages[0][:])
+        nc.sync.dma_start(out=out[P : 2 * P, :], in_=pages[1][:])

from contextlib import ExitStack

import concourse.mybir as mybir

K, T, J, R, O, N, E = 512, 1024, 256, 512, 128, 256, 1024
FLOPS = 2 * (2 * K * R * J) + 2 * R * N * O

F32 = mybir.dt.float32
BF16 = mybir.dt.bfloat16
I32 = mybir.dt.int32
U32 = mybir.dt.uint32
U16 = mybir.dt.uint16
U8 = mybir.dt.uint8
E4M3 = mybir.dt.float8_e4m3fn_x4
E5M2 = mybir.dt.float8_e5m2_x4
E2M1 = mybir.dt.float4_e2m1fn_x4
ACT = mybir.ActivationFunctionType
MULT = mybir.AluOpType.mult

P = 128
PACK = 4
QUADS = 4
QUAD = P // QUADS
LIVE = 4
GROUP = 16
LINE = 4
HALF = O // 2


def tile_list_twow_gatefetch_one_scattered_kernel(
    tc, xt_words, xt_scales, w_words, w_scales, w2_words, w2_scales, sg, bg, wb_words, wb_scales, offs, offs2, offs3, offs4, out
):
    nc = tc.nc
    with ExitStack() as ctx:
        keep = ctx.enter_context(tc.tile_pool(name="keep", bufs=1))
        psum = ctx.enter_context(tc.psum_pool(name="psum", bufs=1))

        def sbuf(name, cols, dtype):
            return keep.tile([P, cols], dtype, name=name, align_bytes=64)

        tokens = sbuf("tokens", J // GROUP, U16)
        gate_slots = sbuf("gate_slots", O // GROUP, U16)
        value_slots = sbuf("value_slots", O // GROUP, U16)
        page_cols = sbuf("page_cols", O // GROUP, U16)
        x_words = sbuf("x_words", T, U32)
        x_plane = sbuf("x_plane", T, U8)
        w_raw = sbuf("w_raw", 2 * R, U8)
        w2_raw = sbuf("w2_raw", R, U32)
        wb_codes = sbuf("wb_codes", N, U32)
        planes = sbuf("planes", 2 * R + N, U8)
        w_plane, w2_plane, wb_plane = planes[:, 0:R], planes[:, R : 2 * R], planes[:, 2 * R :]
        slope = sbuf("slope", PACK, F32)
        shift = sbuf("shift", PACK, F32)
        xg_words = sbuf("xg_words", J, U32)
        xg_plane = sbuf("xg_plane", J, U8)
        w_dealt = sbuf("w_dealt", 2 * R, U8)
        w2_dealt = sbuf("w2_dealt", R, U32)
        w_plane_dealt = sbuf("w_plane_dealt", R, U8)
        w2_plane_dealt = sbuf("w2_plane_dealt", R, U8)
        a_slices = [sbuf("a%d" % t, J, F32) for t in range(PACK)]
        b_slices = [sbuf("b%d" % t, J, F32) for t in range(PACK)]
        gate = sbuf("gate", PACK * O, F32)
        value = sbuf("value", PACK * O, F32)
        hid = sbuf("hid", PACK * O, BF16)
        hid_words = sbuf("hid_words", O, U32)
        hid_plane = sbuf("hid_plane", O, U8)
        p_tiles = [sbuf("p%d" % n, O, F32) for n in range(N // P)]
        pages = [sbuf("page%d" % n, E, F32) for n in range(N // P)]
        warm_in = sbuf("warm_in", 16, F32)
        warm_out = sbuf("warm_out", 16, F32)

        nc.vector.memset(w_plane.bitcast(I32), 0)
        nc.vector.memset(planes[:, R:].bitcast(I32), 0)
        nc.vector.memset(warm_in[:, 0:1], 0.0)
        for page in pages:
            nc.vector.memset(page[:], 0.0)

        def load_rows(queue, plane, scales, q):
            queue.dma_start(
                out=plane[QUAD * q : QUAD * q + LIVE, :].bitcast(I32), in_=scales[0, LIVE * q : LIVE * (q + 1), :].bitcast(I32)
            )

        def load_x_rows(queue, q):
            rows = xt_scales[0, LIVE * q : LIVE * (q + 1), :].bitcast(I32)
            queue.dma_start(
                out=x_plane[QUAD * q : QUAD * (q + 1), :].bitcast(I32),
                in_=rows.unsqueeze(0).to_broadcast([QUAD // LIVE, LIVE, T // 4]),
            )

        def load_words(queue, tile, words):
            queue.dma_start(out=tile[:].bitcast(I32), in_=words[0].rearrange("p n t -> p (n t)").bitcast(I32))

        def load_by_slice(tile, column):
            nc.sync.dma_start(out=tile[:], in_=column.rearrange("(p t) o -> p (t o)", t=PACK))

        both_queues = (nc.sync, nc.scalar)
        for q in range(QUADS):
            load_x_rows(both_queues[q % 2], q)
        nc.sync.dma_start(tokens[:], offs)
        load_words(nc.scalar, x_words, xt_words)
        load_words(nc.sync, w2_raw, w2_words)
        nc.sync.dma_start(out=w_raw[:].bitcast(I32), in_=w_words[0].bitcast(I32))
        for q in range(QUADS):
            load_rows(both_queues[q % 2], w2_plane, w2_scales, q)
        for q in range(QUADS // 2):
            load_rows(nc.sync, w_plane, w_scales, q)
        nc.sync.dma_start(value_slots[:], offs3)
        nc.sync.dma_start(gate_slots[:], offs2)
        load_by_slice(slope, sg)
        load_by_slice(shift, bg)
        load_words(nc.sync, wb_codes, wb_words)
        for q in range(QUADS):
            load_rows(nc.sync, wb_plane, wb_scales, q)
        nc.sync.dma_start(page_cols[:], offs4)
        for q in range(QUADS // 2, QUADS):
            load_rows(nc.gpsimd, w_plane, w_scales, q)

        nc.scalar.activation(out=warm_out[:, 0:1], in_=warm_in[:, 0:1], func=ACT.Sigmoid)

        def deal(copy, dealt, raw, first, count):
            slices = slice(first, first + count)
            copy(out=dealt.rearrange("p (t m) -> p t m", t=PACK)[:, slices, :], in_=raw.rearrange("p (m t) -> p t m", t=PACK)[:, slices, :])

        nc.vector.tensor_copy(out=xg_plane[:], in_=x_plane[:].indirect(tokens[:]))
        nc.vector.tensor_copy(out=xg_words[:], in_=x_words[:].indirect(tokens[:]))

        deal(nc.vector.tensor_copy, w2_dealt[:], w2_raw[:], 0, PACK // 2)
        deal(nc.scalar.copy, w2_dealt[:], w2_raw[:], PACK // 2, PACK // 2)
        deal(nc.scalar.copy, w_dealt[:].bitcast(U16), w_raw[:].bitcast(U16), 0, PACK)
        for t in range(PACK):
            deal(nc.vector.tensor_copy, w2_plane_dealt[:], w2_plane, t, 1)
        for first in range(0, PACK, PACK // 2):
            deal(nc.vector.tensor_copy, w_plane_dealt[:], w_plane, first, PACK // 2)

        def first_product(bank_number, codes, plane):
            bank = psum.tile([P, J], F32, name="bank%d" % bank_number)
            nc.tensor.matmul_mx(
                out=bank[:], lhsT=codes, lhsT_scale=plane, rhs=xg_words[:].bitcast(E4M3), rhs_scale=xg_plane[:], start=True, stop=True
            )
            return bank

        def fetch_gate(t, first, count):
            nc.scalar.activation(
                out=gate[:, O * t + first : O * t + first + count],
                in_=a_slices[t][:].indirect(gate_slots[:, first // GROUP : (first + count) // GROUP]),
                func=ACT.Sigmoid,
                bias=shift[:, t : t + 1],
                scale=slope[:, t : t + 1],
            )

        def multiply(pair, first, count):
            lines = slice(first // LINE, (first + count) // LINE)
            by_slice = "p (u v c i) -> p u c v i"
            nc.vector.tensor_tensor(
                out=hid[:].rearrange("p (c i u v) -> p u c v i", i=LINE, u=2, v=2)[:, pair, lines],
                in0=value[:].rearrange(by_slice, i=LINE, u=2, v=2)[:, pair, lines],
                in1=gate[:].rearrange(by_slice, i=LINE, u=2, v=2)[:, pair, lines],
                op=MULT,
            )

        last = PACK - 1
        for t in range(PACK):
            places = slice(P * t, P * (t + 1))
            bank = first_product(PACK + t, w2_dealt[:, places].bitcast(E5M2), w2_plane_dealt[:, places])
            nc.scalar.copy(out=b_slices[t][:], in_=bank[:])
        for t in range(PACK):
            bank = first_product(t, w_dealt[:, 2 * P * t : 2 * P * (t + 1)].bitcast(E2M1), w_plane_dealt[:, P * t : P * (t + 1)])
            nc.vector.tensor_copy(out=a_slices[t][:], in_=bank[:])
            if t < last:
                fetch_gate(t, 0, O)
        for t in range(PACK // 2):
            nc.vector.tensor_copy(out=value[:, O * t : O * (t + 1)], in_=b_slices[t][:].indirect(value_slots[:]))
        for t in range(PACK // 2, PACK):
            nc.scalar.activation(out=value[:, O * t : O * (t + 1)], in_=b_slices[t][:].indirect(value_slots[:]), func=ACT.Copy)
        multiply(0, 0, O)

        halves = range(0, O, HALF)
        for first in halves:
            fetch_gate(last, first, HALF)
        for first in halves:
            multiply(1, first, HALF)
        for first in halves:
            nc.vector.quantize_mx(
                out=hid_words[:, first : first + HALF].bitcast(E4M3),
                scales=hid_plane[:, first : first + HALF],
                in_=hid[:, PACK * first : PACK * (first + HALF)],
            )

        for n, copy_out in enumerate((nc.scalar.copy, nc.vector.tensor_copy)):
            features = slice(P * n, P * (n + 1))
            bank = psum.tile([P, O], F32, name="bank%d" % n)
            nc.tensor.matmul_mx(
                out=bank[:],
                lhsT=wb_codes[:, features].bitcast(E5M2),
                lhsT_scale=wb_plane[:, features],
                rhs=hid_words[:].bitcast(E4M3),
                rhs_scale=hid_plane[:],
                start=True,
                stop=True,
            )
            copy_out(out=p_tiles[n][:], in_=bank[:])
        nc.scalar.activation(out=pages[0][:].indirect(page_cols[:]), in_=p_tiles[0][:], func=ACT.Copy)
        nc.vector.tensor_copy(out=pages[1][:].indirect(page_cols[:]), in_=p_tiles[1][:])
        nc.scalar.dma_start(out=out[0:P, :], in_=pages[0][:])
        nc.sync.dma_start(out=out[P : 2 * P, :], in_=pages[1][:])
